import numpy as np
import ml_dtypes


def mxq(x, axis, fmt="e4m3"):
    dtype, down = {"e4m3": (ml_dtypes.float8_e4m3fn, 7), "e5m2": (ml_dtypes.float8_e5m2, 14)}[fmt]
    v = np.moveaxis(np.asarray(x, np.float32).astype(ml_dtypes.bfloat16).astype(np.float64), axis, -1)
    blocks = v.reshape(v.shape[:-1] + (-1, 32))
    amax = np.abs(blocks).max(-1, keepdims=True)
    byte = np.maximum(np.where(amax > 0, np.frexp(amax)[1] - 1 + 127, 0) - down, 1)
    scale = np.exp2(byte - 127.0)
    codes = (blocks / scale).astype(np.float32).astype(dtype).astype(np.float64)
    return np.moveaxis((codes * scale).reshape(v.shape), -1, axis)


WIDE = False


def mx_kscale(k):
    if not WIDE:
        return np.ones(k)
    levels = np.array([30, -30])
    if k % 512:
        return np.exp2(np.random.permutation(np.resize(levels, k // 32))).repeat(32)
    a = np.empty((k // 512, 16))
    for p in range(k // 512):
        a[p, :8] = np.random.permutation(np.resize(levels, 8))
        for g in range(8):
            far = levels[np.abs(levels - a[p, g]) >= 10]
            a[p, g + 8] = far[np.random.randint(len(far))]
    return np.exp2(a.ravel()).repeat(32)


def f64(x):
    return np.asarray(x).astype(np.float64)


def striped(idx):
    return np.tile(np.asarray(idx).reshape(-1, 16).T, (8, 1)).astype(np.uint16)


def unstriped(offs):
    return offs[:16].T.reshape(-1).astype(np.int64)


E2M1 = np.array([0.0, 0.5, 1.0, 1.5, 2.0, 3.0, 4.0, 6.0, -0.0, -0.5, -1.0, -1.5, -2.0, -3.0, -4.0, -6.0])


def pack_weight(w, fmt):
    k, n = w.shape
    w = f64(np.asarray(w, np.float32).astype(ml_dtypes.bfloat16)).reshape(k // 32, 32, n)
    amax = np.abs(w).max(1)
    if fmt in ("e4m3", "e5m2"):
        byte = np.frexp(amax)[1] - 1 + 127 - (7 if fmt == "e4m3" else 14)
    else:
        mant, ex = np.frexp(amax / 6.0)
        byte = np.where(mant > 0.5, ex, ex - 1) + 127
    byte = np.clip(np.where(amax > 0, byte, 1), 1, 254)
    scaled = (w * np.exp2(127.0 - byte)[:, None, :]).reshape(k, n).astype(np.float32)
    by_word = np.ascontiguousarray(scaled.reshape(k // 512, 128, 4, n).transpose(0, 1, 3, 2))
    if fmt in ("e4m3", "e5m2"):
        words = by_word.astype(ml_dtypes.float8_e4m3fn if fmt == "e4m3" else ml_dtypes.float8_e5m2).view(np.uint8)
    else:
        c = by_word.astype(ml_dtypes.float4_e2m1fn).view(np.uint8) & 0xF
        words = (c[..., 0::2] | (c[..., 1::2] << 4)).reshape(k // 512, 128, 2 * n)
    return np.ascontiguousarray(words), np.ascontiguousarray(byte.astype(np.uint8).reshape(k // 512, 16, n))


def unpack_weight(words, scales, fmt):
    g, _, n = scales.shape
    words = np.ascontiguousarray(words).reshape(g, 128, n, -1)
    if fmt in ("e4m3", "e5m2"):
        vals = words.view(ml_dtypes.float8_e4m3fn if fmt == "e4m3" else ml_dtypes.float8_e5m2).astype(np.float64)
    else:
        nib = np.empty((g, 128, n, 4), np.uint8)
        nib[..., 0::2] = words & 0xF
        nib[..., 1::2] = words >> 4
        vals = E2M1[nib]
    vals = vals * np.repeat(np.exp2(scales.astype(np.float64) - 127.0), 8, axis=1)[..., None]
    return vals.transpose(0, 1, 3, 2).reshape(g * 512, n)


K, T, Z, J, R, N, E = 512, 1024, 1024, 256, 512, 256, 128


def setup_inputs():
    n = np.random.standard_normal
    idx = np.random.permutation(T)[:J]
    idx2 = np.random.permutation(Z)[:J]
    idx3 = np.random.permutation(J)[:E]
    idx4 = np.random.permutation(J)[:E]
    fk = mx_kscale(K)
    fr = mx_kscale(R)
    xtp = pack_weight(n((K, T)) / fk[:, None], "e5m2")
    xop = pack_weight(n((K, Z)) / fk[:, None], "e4m3")
    wp = pack_weight(n((K, R)) * 1 / np.sqrt(K) * fk[:, None] * fr, "e2m1")
    w2p = pack_weight(n((K, R)) * 1 / np.sqrt(K) * fk[:, None] * fr, "e5m2")
    wbp = pack_weight(n((R, N)) * 1 / np.sqrt(R) / fr[:, None], "e2m1")
    return {
        "xt_words": xtp[0],
        "xt_scales": xtp[1],
        "xo_words": xop[0],
        "xo_scales": xop[1],
        "w_words": wp[0],
        "w_scales": wp[1],
        "w2_words": w2p[0],
        "w2_scales": w2p[1],
        "wb_words": wbp[0],
        "wb_scales": wbp[1],
        "offs": striped(idx),
        "offs2": striped(idx2),
        "offs3": striped(idx3),
        "offs4": striped(idx4),
    }


def reference(xt_words, xt_scales, xo_words, xo_scales, w_words, w_scales, w2_words, w2_scales, wb_words, wb_scales, offs, offs2, offs3, offs4):
    idx = unstriped(offs)
    idx2 = unstriped(offs2)
    idx3 = unstriped(offs3)
    idx4 = unstriped(offs4)
    xtu = unpack_weight(xt_words, xt_scales, "e5m2")
    xou = unpack_weight(xo_words, xo_scales, "e4m3")
    wu = unpack_weight(w_words, w_scales, "e2m1")
    w2u = unpack_weight(w2_words, w2_scales, "e5m2")
    wbu = unpack_weight(wb_words, wb_scales, "e2m1")
    xtidxg = xtu[:, idx]
    xoidx2g = xou[:, idx2]
    a = wu.T @ xtidxg + w2u.T @ xoidx2g
    b = w2u.T @ xtidxg + wu.T @ xoidx2g
    hid = np.abs(a - b)
    hidq = mxq(hid, 0, "e4m3")
    p = wbu.T @ hidq
    y = np.maximum(p[:, idx3], p[:, idx4])
    return y

@@ -1,0 +1,168 @@
+from contextlib import ExitStack
+
+import concourse.mybir as mybir
+
+K, T, Z, J, R, N, E = 512, 1024, 1024, 256, 512, 256, 128
+FLOPS = 2 * (4 * K * R * J + R * N * J)
+
+F32 = mybir.dt.float32
+BF16 = mybir.dt.bfloat16
+I32 = mybir.dt.int32
+U32 = mybir.dt.uint32
+U16 = mybir.dt.uint16
+U8 = mybir.dt.uint8
+E4M3 = mybir.dt.float8_e4m3fn_x4
+E5M2 = mybir.dt.float8_e5m2_x4
+E2M1 = mybir.dt.float4_e2m1fn_x4
+ACT = mybir.ActivationFunctionType
+ALU = mybir.AluOpType
+
+P = 128
+PACK = 4
+HALF = J // 2
+
+
+def load_scale_rows(queue, plane, rows, quadrants=range(4)):
+    for q in quadrants:
+        queue.dma_start(out=plane[32 * q : 32 * q + 4, :].bitcast(I32), in_=rows[0, 4 * q : 4 * q + 4, :].bitcast(I32))
+
+
+def tile_list_crossed_direct_one_bestoftwo_kernel(
+    tc, xt_words, xt_scales, xo_words, xo_scales, w_words, w_scales, w2_words, w2_scales, wb_words, wb_scales, offs, offs2, offs3, offs4, out
+):
+    nc = tc.nc
+    with ExitStack() as ctx:
+        sb = ctx.enter_context(tc.tile_pool(name="sb", bufs=1))
+        ps = ctx.enter_context(tc.psum_pool(name="ps", bufs=1))
+
+        def tile(name, shape, dtype):
+            return sb.tile(shape, dtype, name=name, align_bytes=64)
+
+        idx = tile("idx", [P, J // 16], U16)
+        idx2 = tile("idx2", [P, J // 16], U16)
+        idx3 = tile("idx3", [P, E // 16], U16)
+        idx4 = tile("idx4", [P, E // 16], U16)
+        xt_table = tile("xt_table", [P, T], U32)
+        xo_table = tile("xo_table", [P, Z], U32)
+        xt_plane = tile("xt_plane", [P, T], U8)
+        xo_plane = tile("xo_plane", [P, Z], U8)
+        w_raw = tile("w_raw", [P, 2 * R], U8)
+        w2_raw = tile("w2_raw", [P, R], U32)
+        w_planes_raw = tile("w_planes_raw", [P, 2 * R], U8)
+        wb_codes = tile("wb_codes", [P, 2 * N], U8)
+        wb_plane = tile("wb_plane", [P, N], U8)
+
+        nc.vector.memset(xt_plane[:].bitcast(I32), 0)
+        nc.vector.memset(xo_plane[:].bitcast(I32), 0)
+        nc.vector.memset(w_planes_raw[:].bitcast(I32), 0)
+        nc.vector.memset(wb_plane[:].bitcast(I32), 0)
+
+        nc.sync.dma_start(out=w_raw[:].bitcast(I32), in_=w_words[0].bitcast(I32))
+        nc.sync.dma_start(out=w2_raw[:].bitcast(I32), in_=w2_words[0].rearrange("p n t -> p (n t)").bitcast(I32))
+        nc.sync.dma_start(idx[:], offs)
+        load_scale_rows(nc.sync, xt_plane, xt_scales)
+        nc.sync.dma_start(out=xt_table[:].bitcast(I32), in_=xt_words[0].rearrange("p n t -> p (n t)").bitcast(I32))
+        load_scale_rows(nc.sync, w_planes_raw[:, 0:R], w_scales)
+        nc.sync.dma_start(out=xo_table[:].bitcast(I32), in_=xo_words[0].rearrange("p n t -> p (n t)").bitcast(I32))
+        load_scale_rows(nc.gpsimd, xo_plane, xo_scales)
+        load_scale_rows(nc.sync, w_planes_raw[:, R : 2 * R], w2_scales)
+        nc.sync.dma_start(idx2[:], offs2)
+        nc.sync.dma_start(out=wb_codes[:].bitcast(I32), in_=wb_words[0].bitcast(I32))
+        load_scale_rows(nc.sync, wb_plane, wb_scales)
+        nc.sync.dma_start(idx3[:], offs3)
+        nc.sync.dma_start(idx4[:], offs4)
+
+        w2_codes = tile("w2_codes", [P, PACK, P], U32)
+        w_codes = tile("w_codes", [P, PACK, 2 * P], U8)
+        w_planes = tile("w_planes", [P, PACK, 2, P], U8)
+        xt_codes = tile("xt_codes", [P, J], U32)
+        xt_bytes = tile("xt_bytes", [P, J], U8)
+        xo_codes = [tile(f"xo_codes{h}", [P, HALF], U32) for h in range(2)]
+        xo_bytes = tile("xo_bytes", [P, J], U8)
+
+        nc.scalar.copy(
+            out=w_codes[:].bitcast(U16).rearrange("p t (c i) -> p c t i", i=8),
+            in_=w_raw[:].bitcast(U16).rearrange("p (c i t) -> p c t i", i=8, t=PACK),
+        )
+        nc.scalar.copy(
+            out=w2_codes[:].rearrange("p t (c i) -> p c t i", i=4),
+            in_=w2_raw[:].rearrange("p (c i t) -> p c t i", i=4, t=PACK),
+        )
+        nc.vector.tensor_copy(xt_bytes[:], xt_plane[:].indirect(idx[:]))
+        nc.vector.tensor_copy(xt_codes[:], xt_table[:].indirect(idx[:]))
+        nc.vector.tensor_copy(
+            out=w_planes[:, :, 0, :].rearrange("p t (c i) -> p c t i", i=16),
+            in_=w_planes_raw[:, 0:R].rearrange("p (c i t) -> p c t i", i=16, t=PACK),
+        )
+        nc.vector.tensor_copy(
+            out=w_planes[:, :, 1, :].rearrange("p t (c i) -> p c t i", i=16),
+            in_=w_planes_raw[:, R : 2 * R].rearrange("p (c i t) -> p c t i", i=16, t=PACK),
+        )
+        nc.vector.tensor_copy(xo_bytes[:], xo_plane[:].indirect(idx2[:]))
+        for h in range(2):
+            nc.vector.tensor_copy(xo_codes[h][:], xo_table[:].indirect(idx2[:, 8 * h : 8 * h + 8]))
+
+        a = [ps.tile([P, PACK, HALF], F32, name=f"a{h}") for h in range(2)]
+        b = [ps.tile([P, PACK, HALF], F32, name=f"b{h}") for h in range(2)]
+
+        def with_w(t):
+            return w_codes[:, t, :].bitcast(E2M1), w_planes[:, t, 0, :]
+
+        def with_w2(t):
+            return w2_codes[:, t, :].bitcast(E5M2), w_planes[:, t, 1, :]
+
+        def passes(bank, weight, codes, scale_bytes, first):
+            for t in range(PACK):
+                lhs, lhs_scale = weight(t)
+                nc.tensor.matmul_mx(
+                    out=bank[:, t, :], lhsT=lhs, lhsT_scale=lhs_scale, rhs=codes, rhs_scale=scale_bytes,
+                    start=(first and t == 0), stop=(not first and t == PACK - 1),
+                )
+
+        for banks, weight in ((a, with_w), (b, with_w2)):
+            for h in range(2):
+                cols = slice(h * HALF, (h + 1) * HALF)
+                passes(banks[h], weight, xt_codes[:, cols].bitcast(E5M2), xt_bytes[:, cols], True)
+        for h in range(2):
+            cols = slice(h * HALF, (h + 1) * HALF)
+            passes(b[h], with_w, xo_codes[h][:].bitcast(E4M3), xo_bytes[:, cols], False)
+            passes(a[h], with_w2, xo_codes[h][:].bitcast(E4M3), xo_bytes[:, cols], False)
+
+        b_sb = [tile(f"b_sb{h}", [P, HALF, PACK], F32) for h in range(2)]
+        diff = [tile(f"diff{h}", [P, HALF, PACK], F32) for h in range(2)]
+        hid = [tile(f"hid{h}", [P, HALF * PACK], BF16) for h in range(2)]
+        hid_codes = [tile(f"hid_codes{h}", [P, HALF], U32) for h in range(2)]
+        hid_bytes = [tile(f"hid_bytes{h}", [P, HALF], U8) for h in range(2)]
+        p_sb = [tile(f"p_sb{m}", [P, J], F32) for m in range(2)]
+        for h in range(2):
+            nc.scalar.activation(out=b_sb[h][:], in_=b[h][:].rearrange("p t j -> p j t"), func=ACT.Copy)
+        for h in range(2):
+            nc.vector.tensor_tensor(out=diff[h][:], in0=a[h][:].rearrange("p t j -> p j t"), in1=b_sb[h][:], op=ALU.subtract)
+            flat = diff[h][:].rearrange("p j t -> p (j t)")
+            split = HALF * PACK if h == 0 else 320
+            nc.scalar.activation(out=hid[h][:, :split], in_=flat[:, :split], func=ACT.Abs)
+        for h in range(2):
+            cols = slice(h * HALF, (h + 1) * HALF)
+            if h == 1:
+                nc.vector.scalar_tensor_tensor(out=hid[h][:, split:], in0=flat[:, split:], scalar=-1.0, in1=flat[:, split:], op0=ALU.mult, op1=ALU.max)
+            nc.vector.quantize_mx(out=hid_codes[h][:].bitcast(E4M3), scales=hid_bytes[h][:], in_=hid[h][:])
+            for m in range(2):
+                p_bank = ps.tile([P, HALF], F32, name=f"p{m}{h}")
+                nc.tensor.matmul_mx(
+                    out=p_bank[:], lhsT=wb_codes[:, 2 * P * m : 2 * P * (m + 1)].bitcast(E2M1), lhsT_scale=wb_plane[:, P * m : P * (m + 1)],
+                    rhs=hid_codes[h][:].bitcast(E4M3), rhs_scale=hid_bytes[h][:], start=True, stop=True,
+                )
+                if m == 0:
+                    nc.scalar.activation(out=p_sb[m][:, cols], in_=p_bank[:], func=ACT.Copy)
+                else:
+                    nc.vector.tensor_copy(out=p_sb[m][:, cols], in_=p_bank[:])
+
+        first = tile("first", [P, 2, E], F32)
+        second = tile("second", [P, 2, E], F32)
+        best = tile("best", [P, 2, E], F32)
+        nc.vector.tensor_copy(first[:, 0, :], p_sb[0][:].indirect(idx3[:]))
+        nc.scalar.activation(second[:, 1, :], p_sb[1][:].indirect(idx4[:]), ACT.Copy)
+        nc.vector.tensor_copy(first[:, 1, :], p_sb[1][:].indirect(idx3[:]))
+        nc.scalar.activation(second[:, 0, :], p_sb[0][:].indirect(idx4[:]), ACT.Copy)
+        nc.vector.tensor_tensor(out=best[:], in0=first[:], in1=second[:], op=ALU.max)
+        nc.sync.dma_start(out=out.rearrange("(m p) e -> p m e", p=P), in_=best[:])

@@ -48,25 +48,28 @@ def tile_list_crossed_direct_one_bestoftwo_kernel(
         xo_plane = tile("xo_plane", [P, Z], U8)
         w_raw = tile("w_raw", [P, 2 * R], U8)
         w2_raw = tile("w2_raw", [P, R], U32)
-        w_planes_raw = tile("w_planes_raw", [P, 2 * R], U8)
+        w_plane_raw = tile("w_plane_raw", [P, R], U8)
+        w2_plane_raw = tile("w2_plane_raw", [P, R], U8)
         wb_codes = tile("wb_codes", [P, 2 * N], U8)
         wb_plane = tile("wb_plane", [P, N], U8)
 
         nc.vector.memset(xt_plane[:].bitcast(I32), 0)
+        nc.gpsimd.memset(w2_plane_raw[:].bitcast(I32), 0)
+        nc.vector.memset(w_plane_raw[:].bitcast(I32), 0)
         nc.vector.memset(xo_plane[:].bitcast(I32), 0)
-        nc.vector.memset(w_planes_raw[:].bitcast(I32), 0)
         nc.vector.memset(wb_plane[:].bitcast(I32), 0)
 
         nc.sync.dma_start(out=w_raw[:].bitcast(I32), in_=w_words[0].bitcast(I32))
-        nc.sync.dma_start(out=w2_raw[:].bitcast(I32), in_=w2_words[0].rearrange("p n t -> p (n t)").bitcast(I32))
         nc.sync.dma_start(idx[:], offs)
+        nc.sync.dma_start(out=w2_raw[:].bitcast(I32), in_=w2_words[0].rearrange("p n t -> p (n t)").bitcast(I32))
         load_scale_rows(nc.sync, xt_plane, xt_scales)
         nc.sync.dma_start(out=xt_table[:].bitcast(I32), in_=xt_words[0].rearrange("p n t -> p (n t)").bitcast(I32))
-        load_scale_rows(nc.sync, w_planes_raw[:, 0:R], w_scales)
+        load_scale_rows(nc.gpsimd, w2_plane_raw[:], w2_scales, range(3))
+        load_scale_rows(nc.sync, w_plane_raw[:], w_scales)
+        load_scale_rows(nc.sync, w2_plane_raw[:], w2_scales, range(3, 4))
         nc.sync.dma_start(out=xo_table[:].bitcast(I32), in_=xo_words[0].rearrange("p n t -> p (n t)").bitcast(I32))
-        load_scale_rows(nc.gpsimd, xo_plane, xo_scales)
-        load_scale_rows(nc.sync, w_planes_raw[:, R : 2 * R], w2_scales)
         nc.sync.dma_start(idx2[:], offs2)
+        load_scale_rows(nc.sync, xo_plane, xo_scales)
         nc.sync.dma_start(out=wb_codes[:].bitcast(I32), in_=wb_words[0].bitcast(I32))
         load_scale_rows(nc.sync, wb_plane, wb_scales)
         nc.sync.dma_start(idx3[:], offs3)
@@ -74,11 +77,12 @@ def tile_list_crossed_direct_one_bestoftwo_kernel(
 
         w2_codes = tile("w2_codes", [P, PACK, P], U32)
         w_codes = tile("w_codes", [P, PACK, 2 * P], U8)
-        w_planes = tile("w_planes", [P, PACK, 2, P], U8)
+        w_plane = tile("w_plane", [P, PACK, P], U8)
+        w2_plane = tile("w2_plane", [P, PACK, P], U8)
         xt_codes = tile("xt_codes", [P, J], U32)
         xt_bytes = tile("xt_bytes", [P, J], U8)
         xo_codes = [tile(f"xo_codes{h}", [P, HALF], U32) for h in range(2)]
-        xo_bytes = tile("xo_bytes", [P, J], U8)
+        xo_bytes = [tile(f"xo_bytes{h}", [P, HALF], U8) for h in range(2)]
 
         nc.scalar.copy(
             out=w_codes[:].bitcast(U16).rearrange("p t (c i) -> p c t i", i=8),
@@ -91,25 +95,25 @@ def tile_list_crossed_direct_one_bestoftwo_kernel(
         nc.vector.tensor_copy(xt_bytes[:], xt_plane[:].indirect(idx[:]))
         nc.vector.tensor_copy(xt_codes[:], xt_table[:].indirect(idx[:]))
         nc.vector.tensor_copy(
-            out=w_planes[:, :, 0, :].rearrange("p t (c i) -> p c t i", i=16),
-            in_=w_planes_raw[:, 0:R].rearrange("p (c i t) -> p c t i", i=16, t=PACK),
+            out=w_plane[:].rearrange("p t (c i) -> p c t i", i=16),
+            in_=w_plane_raw[:].rearrange("p (c i t) -> p c t i", i=16, t=PACK),
         )
         nc.vector.tensor_copy(
-            out=w_planes[:, :, 1, :].rearrange("p t (c i) -> p c t i", i=16),
-            in_=w_planes_raw[:, R : 2 * R].rearrange("p (c i t) -> p c t i", i=16, t=PACK),
+            out=w2_plane[:].rearrange("p t (c i) -> p c t i", i=16),
+            in_=w2_plane_raw[:].rearrange("p (c i t) -> p c t i", i=16, t=PACK),
         )
-        nc.vector.tensor_copy(xo_bytes[:], xo_plane[:].indirect(idx2[:]))
         for h in range(2):
             nc.vector.tensor_copy(xo_codes[h][:], xo_table[:].indirect(idx2[:, 8 * h : 8 * h + 8]))
+            nc.vector.tensor_copy(xo_bytes[h][:], xo_plane[:].indirect(idx2[:, 8 * h : 8 * h + 8]))
 
         a = [ps.tile([P, PACK, HALF], F32, name=f"a{h}") for h in range(2)]
         b = [ps.tile([P, PACK, HALF], F32, name=f"b{h}") for h in range(2)]
 
         def with_w(t):
-            return w_codes[:, t, :].bitcast(E2M1), w_planes[:, t, 0, :]
+            return w_codes[:, t, :].bitcast(E2M1), w_plane[:, t, :]
 
         def with_w2(t):
-            return w2_codes[:, t, :].bitcast(E5M2), w_planes[:, t, 1, :]
+            return w2_codes[:, t, :].bitcast(E5M2), w2_plane[:, t, :]
 
         def passes(bank, weight, codes, scale_bytes, first):
             for t in range(PACK):
@@ -125,8 +129,8 @@ def tile_list_crossed_direct_one_bestoftwo_kernel(
                 passes(banks[h], weight, xt_codes[:, cols].bitcast(E5M2), xt_bytes[:, cols], True)
         for h in range(2):
             cols = slice(h * HALF, (h + 1) * HALF)
-            passes(b[h], with_w, xo_codes[h][:].bitcast(E4M3), xo_bytes[:, cols], False)
-            passes(a[h], with_w2, xo_codes[h][:].bitcast(E4M3), xo_bytes[:, cols], False)
+            passes(b[h], with_w, xo_codes[h][:].bitcast(E4M3), xo_bytes[h][:], False)
+            passes(a[h], with_w2, xo_codes[h][:].bitcast(E4M3), xo_bytes[h][:], False)
 
         b_sb = [tile(f"b_sb{h}", [P, HALF, PACK], F32) for h in range(2)]
         diff = [tile(f"diff{h}", [P, HALF, PACK], F32) for h in range(2)]

@@ -49,27 +49,29 @@ def tile_list_crossed_direct_one_bestoftwo_kernel(
         w_raw = tile("w_raw", [P, 2 * R], U8)
         w2_raw = tile("w2_raw", [P, R], U32)
         w_plane_raw = tile("w_plane_raw", [P, R], U8)
-        w2_plane_raw = tile("w2_plane_raw", [P, R], U8)
+        w2_plane_raw = sb.tile([P, R], U8, name="w2_plane_raw", tag="reused", align_bytes=64)
         wb_codes = tile("wb_codes", [P, 2 * N], U8)
         wb_plane = tile("wb_plane", [P, N], U8)
 
         nc.vector.memset(xt_plane[:].bitcast(I32), 0)
-        nc.gpsimd.memset(w2_plane_raw[:].bitcast(I32), 0)
-        nc.vector.memset(w_plane_raw[:].bitcast(I32), 0)
+        nc.gpsimd.memset(w_plane_raw[:].bitcast(I32), 0)
+        nc.vector.memset(w2_plane_raw[:].bitcast(I32), 0)
         nc.vector.memset(xo_plane[:].bitcast(I32), 0)
         nc.vector.memset(wb_plane[:].bitcast(I32), 0)
 
-        nc.sync.dma_start(out=w_raw[:].bitcast(I32), in_=w_words[0].bitcast(I32))
-        nc.sync.dma_start(idx[:], offs)
         nc.sync.dma_start(out=w2_raw[:].bitcast(I32), in_=w2_words[0].rearrange("p n t -> p (n t)").bitcast(I32))
+        nc.sync.dma_start(idx[:], offs)
         load_scale_rows(nc.sync, xt_plane, xt_scales)
+        load_scale_rows(nc.sync, w2_plane_raw[:], w2_scales, [0])
         nc.sync.dma_start(out=xt_table[:].bitcast(I32), in_=xt_words[0].rearrange("p n t -> p (n t)").bitcast(I32))
-        load_scale_rows(nc.gpsimd, w2_plane_raw[:], w2_scales, range(3))
-        load_scale_rows(nc.sync, w_plane_raw[:], w_scales)
-        load_scale_rows(nc.sync, w2_plane_raw[:], w2_scales, range(3, 4))
+        load_scale_rows(nc.gpsimd, w_plane_raw[:], w_scales, range(2))
+        load_scale_rows(nc.gpsimd, xo_plane, xo_scales, [0])
+        load_scale_rows(nc.sync, w2_plane_raw[:], w2_scales, range(1, 4))
+        nc.sync.dma_start(out=w_raw[:].bitcast(I32), in_=w_words[0].bitcast(I32))
+        load_scale_rows(nc.sync, w_plane_raw[:], w_scales, range(2, 4))
         nc.sync.dma_start(out=xo_table[:].bitcast(I32), in_=xo_words[0].rearrange("p n t -> p (n t)").bitcast(I32))
         nc.sync.dma_start(idx2[:], offs2)
-        load_scale_rows(nc.sync, xo_plane, xo_scales)
+        load_scale_rows(nc.sync, xo_plane, xo_scales, range(1, 4))
         nc.sync.dma_start(out=wb_codes[:].bitcast(I32), in_=wb_words[0].bitcast(I32))
         load_scale_rows(nc.sync, wb_plane, wb_scales)
         nc.sync.dma_start(idx3[:], offs3)
@@ -79,31 +81,34 @@ def tile_list_crossed_direct_one_bestoftwo_kernel(
         w_codes = tile("w_codes", [P, PACK, 2 * P], U8)
         w_plane = tile("w_plane", [P, PACK, P], U8)
         w2_plane = tile("w2_plane", [P, PACK, P], U8)
-        xt_codes = tile("xt_codes", [P, J], U32)
+        xt_codes = [tile("xt_codes0", [P, HALF], U32)]
         xt_bytes = tile("xt_bytes", [P, J], U8)
         xo_codes = [tile(f"xo_codes{h}", [P, HALF], U32) for h in range(2)]
         xo_bytes = [tile(f"xo_bytes{h}", [P, HALF], U8) for h in range(2)]
 
         nc.scalar.copy(
-            out=w_codes[:].bitcast(U16).rearrange("p t (c i) -> p c t i", i=8),
-            in_=w_raw[:].bitcast(U16).rearrange("p (c i t) -> p c t i", i=8, t=PACK),
-        )
-        nc.scalar.copy(
             out=w2_codes[:].rearrange("p t (c i) -> p c t i", i=4),
             in_=w2_raw[:].rearrange("p (c i t) -> p c t i", i=4, t=PACK),
         )
-        nc.vector.tensor_copy(xt_bytes[:], xt_plane[:].indirect(idx[:]))
-        nc.vector.tensor_copy(xt_codes[:], xt_table[:].indirect(idx[:]))
-        nc.vector.tensor_copy(
-            out=w_plane[:].rearrange("p t (c i) -> p c t i", i=16),
-            in_=w_plane_raw[:].rearrange("p (c i t) -> p c t i", i=16, t=PACK),
+        nc.scalar.copy(
+            out=w_codes[:].bitcast(U16).rearrange("p t (c i) -> p c t i", i=8),
+            in_=w_raw[:].bitcast(U16).rearrange("p (c i t) -> p c t i", i=8, t=PACK),
         )
+        nc.vector.tensor_copy(xt_bytes[:], xt_plane[:].indirect(idx[:]))
+        nc.vector.tensor_copy(xt_codes[0][:], xt_table[:].indirect(idx[:, 0:8]))
         nc.vector.tensor_copy(
             out=w2_plane[:].rearrange("p t (c i) -> p c t i", i=16),
             in_=w2_plane_raw[:].rearrange("p (c i t) -> p c t i", i=16, t=PACK),
         )
+        xt_codes.append(sb.tile([P, HALF], U32, name="xt_codes1", tag="reused", align_bytes=64))
+        nc.vector.tensor_copy(xt_codes[1][:], xt_table[:].indirect(idx[:, 8:16]))
+        nc.vector.tensor_copy(
+            out=w_plane[:].rearrange("p t (c i) -> p c t i", i=16),
+            in_=w_plane_raw[:].rearrange("p (c i t) -> p c t i", i=16, t=PACK),
+        )
         for h in range(2):
             nc.vector.tensor_copy(xo_codes[h][:], xo_table[:].indirect(idx2[:, 8 * h : 8 * h + 8]))
+        for h in range(2):
             nc.vector.tensor_copy(xo_bytes[h][:], xo_plane[:].indirect(idx2[:, 8 * h : 8 * h + 8]))
 
         a = [ps.tile([P, PACK, HALF], F32, name=f"a{h}") for h in range(2)]
@@ -123,10 +128,10 @@ def tile_list_crossed_direct_one_bestoftwo_kernel(
                     start=(first and t == 0), stop=(not first and t == PACK - 1),
                 )
 
-        for banks, weight in ((a, with_w), (b, with_w2)):
+        for banks, weight in ((b, with_w2), (a, with_w)):
             for h in range(2):
                 cols = slice(h * HALF, (h + 1) * HALF)
-                passes(banks[h], weight, xt_codes[:, cols].bitcast(E5M2), xt_bytes[:, cols], True)
+                passes(banks[h], weight, xt_codes[h][:].bitcast(E5M2), xt_bytes[:, cols], True)
         for h in range(2):
             cols = slice(h * HALF, (h + 1) * HALF)
             passes(b[h], with_w, xo_codes[h][:].bitcast(E4M3), xo_bytes[h][:], False)

from contextlib import ExitStack

import concourse.mybir as mybir

K, T, Z, J, R, N, E = 512, 1024, 1024, 256, 512, 256, 128
FLOPS = 2 * (4 * K * R * J + R * N * J)

F32 = mybir.dt.float32
BF16 = mybir.dt.bfloat16
I32 = mybir.dt.int32
U32 = mybir.dt.uint32
U16 = mybir.dt.uint16
U8 = mybir.dt.uint8
E4M3 = mybir.dt.float8_e4m3fn_x4
E5M2 = mybir.dt.float8_e5m2_x4
E2M1 = mybir.dt.float4_e2m1fn_x4
ACT = mybir.ActivationFunctionType
ALU = mybir.AluOpType

P = 128
PACK = 4
HALF = J // 2


def load_scale_rows(queue, plane, rows, quadrants=range(4)):
    for q in quadrants:
        queue.dma_start(out=plane[32 * q : 32 * q + 4, :].bitcast(I32), in_=rows[0, 4 * q : 4 * q + 4, :].bitcast(I32))


def tile_list_crossed_direct_one_bestoftwo_kernel(
    tc, xt_words, xt_scales, xo_words, xo_scales, w_words, w_scales, w2_words, w2_scales, wb_words, wb_scales, offs, offs2, offs3, offs4, out
):
    nc = tc.nc
    with ExitStack() as ctx:
        sb = ctx.enter_context(tc.tile_pool(name="sb", bufs=1))
        ps = ctx.enter_context(tc.psum_pool(name="ps", bufs=1))

        def tile(name, shape, dtype):
            return sb.tile(shape, dtype, name=name, align_bytes=64)

        idx = tile("idx", [P, J // 16], U16)
        idx2 = tile("idx2", [P, J // 16], U16)
        idx3 = tile("idx3", [P, E // 16], U16)
        idx4 = tile("idx4", [P, E // 16], U16)
        xt_table = tile("xt_table", [P, T], U32)
        xo_table = tile("xo_table", [P, Z], U32)
        xt_plane = tile("xt_plane", [P, T], U8)
        xo_plane = tile("xo_plane", [P, Z], U8)
        w_raw = tile("w_raw", [P, 2 * R], U8)
        w2_raw = tile("w2_raw", [P, R], U32)
        w_plane_raw = tile("w_plane_raw", [P, R], U8)
        w2_plane_raw = sb.tile([P, R], U8, name="w2_plane_raw", tag="reused", align_bytes=64)
        wb_codes = tile("wb_codes", [P, 2 * N], U8)
        wb_plane = tile("wb_plane", [P, N], U8)

        nc.vector.memset(xt_plane[:].bitcast(I32), 0)
        nc.gpsimd.memset(w_plane_raw[:].bitcast(I32), 0)
        nc.vector.memset(w2_plane_raw[:].bitcast(I32), 0)
        nc.vector.memset(xo_plane[:].bitcast(I32), 0)
        nc.vector.memset(wb_plane[:].bitcast(I32), 0)

        nc.sync.dma_start(out=w2_raw[:].bitcast(I32), in_=w2_words[0].rearrange("p n t -> p (n t)").bitcast(I32))
        nc.sync.dma_start(idx[:], offs)
        load_scale_rows(nc.sync, xt_plane, xt_scales)
        load_scale_rows(nc.sync, w2_plane_raw[:], w2_scales, [0])
        nc.sync.dma_start(out=xt_table[:].bitcast(I32), in_=xt_words[0].rearrange("p n t -> p (n t)").bitcast(I32))
        load_scale_rows(nc.gpsimd, w_plane_raw[:], w_scales, range(2))
        load_scale_rows(nc.gpsimd, xo_plane, xo_scales, [0])
        load_scale_rows(nc.sync, w2_plane_raw[:], w2_scales, range(1, 4))
        nc.sync.dma_start(out=w_raw[:].bitcast(I32), in_=w_words[0].bitcast(I32))
        load_scale_rows(nc.sync, w_plane_raw[:], w_scales, range(2, 4))
        nc.sync.dma_start(out=xo_table[:].bitcast(I32), in_=xo_words[0].rearrange("p n t -> p (n t)").bitcast(I32))
        nc.sync.dma_start(idx2[:], offs2)
        load_scale_rows(nc.sync, xo_plane, xo_scales, range(1, 4))
        nc.sync.dma_start(out=wb_codes[:].bitcast(I32), in_=wb_words[0].bitcast(I32))
        load_scale_rows(nc.sync, wb_plane, wb_scales)
        nc.sync.dma_start(idx3[:], offs3)
        nc.sync.dma_start(idx4[:], offs4)

        w2_codes = tile("w2_codes", [P, PACK, P], U32)
        w_codes = tile("w_codes", [P, PACK, 2 * P], U8)
        w_plane = tile("w_plane", [P, PACK, P], U8)
        w2_plane = tile("w2_plane", [P, PACK, P], U8)
        xt_codes = [tile("xt_codes0", [P, HALF], U32)]
        xt_bytes = tile("xt_bytes", [P, J], U8)
        xo_codes = [tile(f"xo_codes{h}", [P, HALF], U32) for h in range(2)]
        xo_bytes = [tile(f"xo_bytes{h}", [P, HALF], U8) for h in range(2)]

        nc.scalar.copy(
            out=w2_codes[:].rearrange("p t (c i) -> p c t i", i=4),
            in_=w2_raw[:].rearrange("p (c i t) -> p c t i", i=4, t=PACK),
        )
        nc.scalar.copy(
            out=w_codes[:].bitcast(U16).rearrange("p t (c i) -> p c t i", i=8),
            in_=w_raw[:].bitcast(U16).rearrange("p (c i t) -> p c t i", i=8, t=PACK),
        )
        nc.vector.tensor_copy(xt_bytes[:], xt_plane[:].indirect(idx[:]))
        nc.vector.tensor_copy(xt_codes[0][:], xt_table[:].indirect(idx[:, 0:8]))
        nc.vector.tensor_copy(
            out=w2_plane[:].rearrange("p t (c i) -> p c t i", i=16),
            in_=w2_plane_raw[:].rearrange("p (c i t) -> p c t i", i=16, t=PACK),
        )
        xt_codes.append(sb.tile([P, HALF], U32, name="xt_codes1", tag="reused", align_bytes=64))
        nc.vector.tensor_copy(xt_codes[1][:], xt_table[:].indirect(idx[:, 8:16]))
        nc.vector.tensor_copy(
            out=w_plane[:].rearrange("p t (c i) -> p c t i", i=16),
            in_=w_plane_raw[:].rearrange("p (c i t) -> p c t i", i=16, t=PACK),
        )
        for h in range(2):
            nc.vector.tensor_copy(xo_codes[h][:], xo_table[:].indirect(idx2[:, 8 * h : 8 * h + 8]))
        for h in range(2):
            nc.vector.tensor_copy(xo_bytes[h][:], xo_plane[:].indirect(idx2[:, 8 * h : 8 * h + 8]))

        a = [ps.tile([P, PACK, HALF], F32, name=f"a{h}") for h in range(2)]
        b = [ps.tile([P, PACK, HALF], F32, name=f"b{h}") for h in range(2)]

        def with_w(t):
            return w_codes[:, t, :].bitcast(E2M1), w_plane[:, t, :]

        def with_w2(t):
            return w2_codes[:, t, :].bitcast(E5M2), w2_plane[:, t, :]

        def passes(bank, weight, codes, scale_bytes, first):
            for t in range(PACK):
                lhs, lhs_scale = weight(t)
                nc.tensor.matmul_mx(
                    out=bank[:, t, :], lhsT=lhs, lhsT_scale=lhs_scale, rhs=codes, rhs_scale=scale_bytes,
                    start=(first and t == 0), stop=(not first and t == PACK - 1),
                )

        for banks, weight in ((b, with_w2), (a, with_w)):
            for h in range(2):
                cols = slice(h * HALF, (h + 1) * HALF)
                passes(banks[h], weight, xt_codes[h][:].bitcast(E5M2), xt_bytes[:, cols], True)
        for h in range(2):
            cols = slice(h * HALF, (h + 1) * HALF)
            passes(b[h], with_w, xo_codes[h][:].bitcast(E4M3), xo_bytes[h][:], False)
            passes(a[h], with_w2, xo_codes[h][:].bitcast(E4M3), xo_bytes[h][:], False)

        b_sb = [tile(f"b_sb{h}", [P, HALF, PACK], F32) for h in range(2)]
        diff = [tile(f"diff{h}", [P, HALF, PACK], F32) for h in range(2)]
        hid = [tile(f"hid{h}", [P, HALF * PACK], BF16) for h in range(2)]
        hid_codes = [tile(f"hid_codes{h}", [P, HALF], U32) for h in range(2)]
        hid_bytes = [tile(f"hid_bytes{h}", [P, HALF], U8) for h in range(2)]
        p_sb = [tile(f"p_sb{m}", [P, J], F32) for m in range(2)]
        for h in range(2):
            nc.scalar.activation(out=b_sb[h][:], in_=b[h][:].rearrange("p t j -> p j t"), func=ACT.Copy)
        for h in range(2):
            nc.vector.tensor_tensor(out=diff[h][:], in0=a[h][:].rearrange("p t j -> p j t"), in1=b_sb[h][:], op=ALU.subtract)
            flat = diff[h][:].rearrange("p j t -> p (j t)")
            split = HALF * PACK if h == 0 else 320
            nc.scalar.activation(out=hid[h][:, :split], in_=flat[:, :split], func=ACT.Abs)
        for h in range(2):
            cols = slice(h * HALF, (h + 1) * HALF)
            if h == 1:
                nc.vector.scalar_tensor_tensor(out=hid[h][:, split:], in0=flat[:, split:], scalar=-1.0, in1=flat[:, split:], op0=ALU.mult, op1=ALU.max)
            nc.vector.quantize_mx(out=hid_codes[h][:].bitcast(E4M3), scales=hid_bytes[h][:], in_=hid[h][:])
            for m in range(2):
                p_bank = ps.tile([P, HALF], F32, name=f"p{m}{h}")
                nc.tensor.matmul_mx(
                    out=p_bank[:], lhsT=wb_codes[:, 2 * P * m : 2 * P * (m + 1)].bitcast(E2M1), lhsT_scale=wb_plane[:, P * m : P * (m + 1)],
                    rhs=hid_codes[h][:].bitcast(E4M3), rhs_scale=hid_bytes[h][:], start=True, stop=True,
                )
                if m == 0:
                    nc.scalar.activation(out=p_sb[m][:, cols], in_=p_bank[:], func=ACT.Copy)
                else:
                    nc.vector.tensor_copy(out=p_sb[m][:, cols], in_=p_bank[:])

        first = tile("first", [P, 2, E], F32)
        second = tile("second", [P, 2, E], F32)
        best = tile("best", [P, 2, E], F32)
        nc.vector.tensor_copy(first[:, 0, :], p_sb[0][:].indirect(idx3[:]))
        nc.scalar.activation(second[:, 1, :], p_sb[1][:].indirect(idx4[:]), ACT.Copy)
        nc.vector.tensor_copy(first[:, 1, :], p_sb[1][:].indirect(idx3[:]))
        nc.scalar.activation(second[:, 0, :], p_sb[0][:].indirect(idx4[:]), ACT.Copy)
        nc.vector.tensor_tensor(out=best[:], in0=first[:], in1=second[:], op=ALU.max)
        nc.sync.dma_start(out=out.rearrange("(m p) e -> p m e", p=P), in_=best[:])
